import numpy as np, ml_dtypes
CORES = [3,0,2,1,6,7,4,5]
N = 8
def setup_inputs(rng):
    return {"x": rng.standard_normal((N, 128, 64), dtype=np.float32).astype(ml_dtypes.bfloat16)}
def reference(x):
    g = np.concatenate(list(x), axis=1).astype(np.float32)
    return {"y": np.broadcast_to(g, (N,) + g.shape)}

from concourse.bass import DstId, RemoteDMATransfer

BLOCK = 64
RANKS = 8
ENGINES = 16

SCRATCH = {
    "gath": ("sbuf", [128, RANKS * BLOCK], "bfloat16"),
    "wide": ("sbuf", [128, RANKS * BLOCK], "float32"),
}
SEMAPHORES = ["loaded", "sent", "arrived", "widened", "stored"]


def rank_program(g, core, T, topo):
    rank = T.rank_of(core)
    if rank is None:
        return

    slot = T.gath[:, rank * BLOCK:(rank + 1) * BLOCK]
    peers = [c for c in T.cores if c != core]

    g.dma_start(slot, T.x[:]).then_inc(T.sem.loaded, 16)
    g.wait_ge(T.sem.loaded, 16)

    dst_ids = []
    mask = 0xFFFF
    for c in peers:
        address = topo.addr(c)
        dst_ids.append(DstId(rid=address[0], pnc=address[1]))
        mask &= topo.mask(core, c)
    g.remote_dma_fused(
        [RemoteDMATransfer(dst_ids=dst_ids, dma_engine_mask=mask, remote_sem=T.sem.arrived,
                           srcs=[slot], dsts=[slot for c in peers], alu_op=0)],
        local_sem=T.sem.sent,
    )

    g.vector.wait_ge(T.sem.loaded, 16)
    g.vector.wait_ge(T.sem.arrived, ENGINES * len(peers))
    g.vector.tensor_copy(T.wide[:], T.gath[:]).then_inc(T.sem.widened, 1)

    g.wait_ge(T.sem.widened, 1)
    g.dma_start(T.y[:], T.wide[:]).then_inc(T.sem.stored, 16)
    g.wait_ge(T.sem.sent, ENGINES)
    g.wait_ge(T.sem.stored, 16)
